import numpy as np
import ml_dtypes


def mxq(x, axis, fmt="e4m3"):
    dtype, down = {"e4m3": (ml_dtypes.float8_e4m3fn, 7), "e5m2": (ml_dtypes.float8_e5m2, 14)}[fmt]
    v = np.moveaxis(np.asarray(x, np.float32).astype(ml_dtypes.bfloat16).astype(np.float64), axis, -1)
    blocks = v.reshape(v.shape[:-1] + (-1, 32))
    amax = np.abs(blocks).max(-1, keepdims=True)
    byte = np.maximum(np.where(amax > 0, np.frexp(amax)[1] - 1 + 127, 0) - down, 1)
    scale = np.exp2(byte - 127.0)
    codes = (blocks / scale).astype(np.float32).astype(dtype).astype(np.float64)
    return np.moveaxis((codes * scale).reshape(v.shape), -1, axis)


WIDE = False


def mx_kscale(k):
    if not WIDE:
        return np.ones(k)
    levels = np.array([24, -24, 12, -12, 0])
    if k % 512:
        return np.exp2(np.random.permutation(np.resize(levels, k // 32))).repeat(32)
    a = np.empty((k // 512, 16))
    for p in range(k // 512):
        a[p, :8] = np.random.permutation(np.resize(levels, 8))
        for g in range(8):
            far = levels[np.abs(levels - a[p, g]) >= 10]
            a[p, g + 8] = far[np.random.randint(len(far))]
    return np.exp2(a.ravel()).repeat(32)


def f64(x):
    return np.asarray(x).astype(np.float64)


def striped(idx):
    return np.tile(idx.reshape(-1, 16).T, (8, 1)).astype(np.uint16)


def unstriped(offs):
    return offs[:16].T.reshape(-1).astype(np.int64)


E2M1 = np.array([0.0, 0.5, 1.0, 1.5, 2.0, 3.0, 4.0, 6.0, -0.0, -0.5, -1.0, -1.5, -2.0, -3.0, -4.0, -6.0])


def pack_weight(w, fmt):
    k, n = w.shape
    w = f64(np.asarray(w, np.float32).astype(ml_dtypes.bfloat16)).reshape(k // 32, 32, n)
    amax = np.abs(w).max(1)
    if fmt == "e4m3":
        byte = np.frexp(amax)[1] - 1 + 127 - 7
    else:
        mant, ex = np.frexp(amax / 6.0)
        byte = np.where(mant > 0.5, ex, ex - 1) + 127
    byte = np.clip(np.where(amax > 0, byte, 1), 1, 254)
    scaled = (w * np.exp2(127.0 - byte)[:, None, :]).reshape(k, n).astype(np.float32)
    by_word = np.ascontiguousarray(scaled.reshape(k // 512, 128, 4, n).transpose(0, 1, 3, 2))
    if fmt == "e4m3":
        words = by_word.astype(ml_dtypes.float8_e4m3fn).view(np.uint8)
    else:
        c = by_word.astype(ml_dtypes.float4_e2m1fn).view(np.uint8) & 0xF
        words = (c[..., 0::2] | (c[..., 1::2] << 4)).reshape(k // 512, 128, 2 * n)
    return np.ascontiguousarray(words), np.ascontiguousarray(byte.astype(np.uint8).reshape(k // 512, 16, n))


def unpack_weight(words, scales, fmt):
    g, _, n = scales.shape
    words = np.ascontiguousarray(words).reshape(g, 128, n, -1)
    if fmt == "e4m3":
        vals = words.view(ml_dtypes.float8_e4m3fn).astype(np.float64)
    else:
        nib = np.empty((g, 128, n, 4), np.uint8)
        nib[..., 0::2] = words & 0xF
        nib[..., 1::2] = words >> 4
        vals = E2M1[nib]
    vals = vals * np.repeat(np.exp2(scales.astype(np.float64) - 127.0), 8, axis=1)[..., None]
    return vals.transpose(0, 1, 3, 2).reshape(g * 512, n)


def sigm(f):
    return 1.0 / (1.0 + np.exp(-np.maximum(f, -700.0)))


K, M, N, T, J = 1024, 512, 512, 2048, 1024


def setup_inputs():
    n = np.random.standard_normal
    s = mx_kscale(K)[:, None]
    s2 = mx_kscale(M)[:, None]
    h = np.tanh(n((N, T)))
    p_tab = pack_weight(h * s2, "e4m3")
    p_wz = pack_weight(n((K, N)) / np.sqrt(K) / s, "e4m3")
    p_uz = pack_weight(n((M, N)) / np.sqrt(M) / s2, "e2m1")
    p_wr = pack_weight(n((K, N)) / np.sqrt(K) / s, "e4m3")
    p_ur = pack_weight(n((M, N)) / np.sqrt(M) / s2, "e2m1")
    p_wn = pack_weight(n((K, N)) / np.sqrt(K) / s, "e4m3")
    p_un = pack_weight(n((M, N)) / np.sqrt(M) / s2, "e2m1")
    return {
        "x": (n((K, J)) * s).astype(np.float32),
        "tab_words": p_tab[0],
        "tab_scales": p_tab[1],
        "wz_words": p_wz[0],
        "wz_scales": p_wz[1],
        "uz_words": p_uz[0],
        "uz_scales": p_uz[1],
        "wr_words": p_wr[0],
        "wr_scales": p_wr[1],
        "ur_words": p_ur[0],
        "ur_scales": p_ur[1],
        "wn_words": p_wn[0],
        "wn_scales": p_wn[1],
        "un_words": p_un[0],
        "un_scales": p_un[1],
        "bz": (0.3 * n(N)).astype(np.float32),
        "br": (0.3 * n(N)).astype(np.float32),
        "bn": (0.3 * n(N)).astype(np.float32),
        "hT": (h).astype(np.float32),
        "wgo": np.tile(np.random.uniform(0.5, 2.0, J), (128, 1)).astype(np.float32),
        "offs": striped(np.random.permutation(T)[:J]),
    }


def reference(x, tab_words, tab_scales, wz_words, wz_scales, uz_words, uz_scales, wr_words, wr_scales, ur_words, ur_scales, wn_words, wn_scales, un_words, un_scales, bz, br, bn, hT, wgo, offs):
    idx = unstriped(offs)
    x_ = mxq(f64(x), 0, "e4m3")
    tab_ = unpack_weight(tab_words, tab_scales, "e4m3")[:, idx]
    wz_ = unpack_weight(wz_words, wz_scales, "e4m3")
    uz_ = unpack_weight(uz_words, uz_scales, "e2m1")
    wr_ = unpack_weight(wr_words, wr_scales, "e4m3")
    ur_ = unpack_weight(ur_words, ur_scales, "e2m1")
    wn_ = unpack_weight(wn_words, wn_scales, "e4m3")
    un_ = unpack_weight(un_words, un_scales, "e2m1")
    sz = wz_.T @ x_ + uz_.T @ tab_
    z = sigm(sz + f64(bz)[:, None])
    sr = wr_.T @ x_ + ur_.T @ tab_
    r = sigm(sr + f64(br)[:, None])
    xn = wn_.T @ x_
    hn = un_.T @ tab_
    cd = np.tanh(xn + f64(bn)[:, None] + r * hn)
    out = np.zeros((N, T))
    out[:, idx] = f64(wgo)[0] * (f64(hT)[:, idx] + z * (cd - f64(hT)[:, idx]))
    return out

@@ -1,0 +1,273 @@
+from contextlib import ExitStack
+
+import concourse.mybir as mybir
+
+K, M, N, T, J = 1024, 512, 512, 2048, 1024
+FLOPS = 2 * 3 * (K + M) * N * J
+
+F32 = mybir.dt.float32
+BF16 = mybir.dt.bfloat16
+I32 = mybir.dt.int32
+U32 = mybir.dt.uint32
+U16 = mybir.dt.uint16
+U8 = mybir.dt.uint8
+FP8X4 = mybir.dt.float8_e4m3fn_x4
+FP4X4 = mybir.dt.float4_e2m1fn_x4
+ALU = mybir.AluOpType
+ACT = mybir.ActivationFunctionType
+
+P = 128
+PACK = 4
+K_PASS = P * PACK
+PASSES = K // K_PASS
+JC = 512
+J_CHUNKS = J // JC
+N_TILES = N // P
+N_HALF = N // 2
+GATES = ("r", "n", "z")
+
+
+def tile_list_tgn_gru_kernel(
+    tc, x, tab_words, tab_scales, wz_words, wz_scales, uz_words, uz_scales, wr_words, wr_scales, ur_words,
+    ur_scales, wn_words, wn_scales, un_words, un_scales, bz, br, bn, hT, wgo, offs, out,
+):
+    nc = tc.nc
+    w_words = {"r": wr_words, "n": wn_words, "z": wz_words}
+    w_scales = {"r": wr_scales, "n": wn_scales, "z": wz_scales}
+    u_words = {"r": ur_words, "n": un_words, "z": uz_words}
+    u_scales = {"r": ur_scales, "n": un_scales, "z": uz_scales}
+    biases = {"r": br, "n": bn, "z": bz}
+
+    with ExitStack() as ctx:
+        keep = ctx.enter_context(tc.tile_pool(name="keep", bufs=1))
+        work = ctx.enter_context(tc.tile_pool(name="work", bufs=3))
+        psum = ctx.enter_context(tc.psum_pool(name="psum", bufs=2))
+
+        offsets = keep.tile([P, J // 16], U16, name="offsets")
+        nc.sync.dma_start(offsets[:], offs)
+
+        def listed(c):
+            return offsets[:, c * JC // 16 : (c + 1) * JC // 16]
+
+        tab_plane = keep.tile([P, T], U8, name="tab_plane", align_bytes=64)
+        nc.vector.memset(tab_plane[:].bitcast(I32), 0)
+        for q in range(4):
+            nc.gpsimd.dma_start(
+                tab_plane[32 * q : 32 * q + 4, :].bitcast(I32), tab_scales[0, 4 * q : 4 * q + 4, :].bitcast(I32)
+            )
+        GATE_COLS = (PASSES + 1) * N
+        w_plane = keep.tile([P, len(GATES) * GATE_COLS], U8, name="w_plane", align_bytes=64)
+        nc.vector.memset(w_plane[:].bitcast(I32), 0)
+        w_rows = keep.tile([16, len(GATES) * GATE_COLS // 4], I32, name="w_rows")
+
+        def load_w_scales(gate):
+            c0 = GATES.index(gate) * GATE_COLS // 4
+            nc.sync.dma_start(
+                w_rows[:, c0 : c0 + PASSES * N // 4].rearrange("q (a n) -> q a n", a=PASSES),
+                w_scales[gate].bitcast(I32).rearrange("a q n -> q a n"),
+            )
+
+        def load_u_scales(gate):
+            c0 = (GATES.index(gate) * GATE_COLS + PASSES * N) // 4
+            nc.sync.dma_start(w_rows[:, c0 : c0 + N // 4], u_scales[gate][0].bitcast(I32))
+
+        bias, half_bias = {}, {}
+
+        def load_bias(gate):
+            bias[gate] = keep.tile([P, N_TILES], F32, name="bias_" + gate)
+            with nc.allow_non_contiguous_dma(reason="one bias value for each partition and tile"):
+                nc.sync.dma_start(bias[gate][:], biases[gate].rearrange("(t p) -> p t", p=P))
+            if gate != "n":
+                half_bias[gate] = keep.tile([P, N_TILES], F32, name="half_bias_" + gate)
+                nc.scalar.mul(half_bias[gate][:], bias[gate][:], 0.5)
+
+        pages = [keep.tile([P, T], F32, name="page%d" % i) for i in range(2)]
+        for page in pages:
+            nc.vector.memset(page[:, 0 : T // 2 - 1], 0.0)
+            nc.vector.memset(page[:, T // 2 - 1 : T], 0.0)
+
+        x_raw, w_codes, u_codes, state, weight = {}, {}, {}, {}, {}
+
+        def load_x(a, c):
+            x_raw[a, c] = keep.tile([P, PACK, JC], F32, name="x_raw%d%d" % (a, c))
+            rows = x[a * K_PASS : (a + 1) * K_PASS, c * JC : (c + 1) * JC]
+            nc.sync.dma_start(x_raw[a, c][:], rows.rearrange("(p i) j -> p i j", i=PACK))
+
+        def load_w(gate, half):
+            w_codes[gate, half] = keep.tile([P, PASSES, N_HALF], I32, name="w_%s%d" % (gate, half), align_bytes=64)
+            words = w_words[gate].rearrange("a p n i -> p a (n i)").bitcast(I32)
+            nc.sync.dma_start(w_codes[gate, half][:], words[:, :, half * N_HALF : (half + 1) * N_HALF])
+
+        def load_u(gate):
+            u_codes[gate] = keep.tile([P, 2 * N], U8, name="u_" + gate, align_bytes=64)
+            nc.sync.dma_start(u_codes[gate][:].bitcast(I32), u_words[gate][0].bitcast(I32))
+
+        def load_state(t):
+            state[t] = keep.tile([P, T], F32, name="state%d" % t)
+            nc.sync.dma_start(state[t][:], hT[t * P : (t + 1) * P, :])
+
+        def load_weight(c):
+            weight[c] = keep.tile([P, JC], F32, name="weight%d" % c)
+            nc.sync.dma_start(weight[c][:], wgo[:, c * JC : (c + 1) * JC])
+
+        tab = keep.tile([P, T], I32, name="tab", align_bytes=64)
+        load_x(0, 0)
+        load_w_scales("r")
+        load_u_scales("r")
+        nc.sync.dma_start(tab[:], tab_words[0].rearrange("p t i -> p (t i)").bitcast(I32))
+        load_w_scales("n")
+        load_u_scales("n")
+        load_w_scales("z")
+        load_u_scales("z")
+        load_x(1, 0)
+        for q in range(4):
+            nc.gpsimd.dma_start(w_plane[32 * q : 32 * q + 4, :].bitcast(I32), w_rows[4 * q : 4 * q + 4, :])
+        for gate in GATES:
+            load_w(gate, 0)
+            load_u(gate)
+        load_bias("r")
+        load_state(0)
+        load_bias("n")
+        load_bias("z")
+        load_weight(0)
+        load_x(0, 1)
+        load_x(1, 1)
+        load_state(1)
+        load_weight(1)
+        for gate in GATES:
+            load_w(gate, 1)
+        load_state(2)
+        load_state(3)
+
+        x_codes, x_plane, v_codes, v_plane = {}, {}, {}, {}
+
+        def quantise_x(a, c, on_vector):
+            grouped = keep.tile([P, JC, PACK], BF16, name="grouped%d%d" % (a, c), align_bytes=64)
+            dst = grouped[:].rearrange("p (g i) t -> p g t i", i=4)
+            src = x_raw[a, c][:].rearrange("p t (g i) -> p g t i", i=4)
+            if on_vector:
+                nc.vector.tensor_copy(dst, src)
+            else:
+                nc.scalar.copy(dst, src)
+            x_codes[a, c] = keep.tile([P, JC], U32, name="x_codes%d%d" % (a, c), align_bytes=64)
+            x_plane[a, c] = keep.tile([P, JC], U8, name="x_plane%d%d" % (a, c), align_bytes=64)
+            nc.vector.quantize_mx(
+                x_codes[a, c][:].bitcast(FP8X4), x_plane[a, c][:], grouped[:].rearrange("p j t -> p (j t)")
+            )
+
+        def gather_table(c):
+            v_codes[c] = keep.tile([P, JC], U32, name="v_codes%d" % c, align_bytes=64)
+            v_plane[c] = keep.tile([P, JC], U8, name="v_plane%d" % c, align_bytes=64)
+            nc.vector.tensor_copy(v_codes[c][:], tab[:].bitcast(U32).indirect(listed(c)))
+            nc.vector.tensor_copy(v_plane[c][:], tab_plane[:].indirect(listed(c)))
+
+        gather_table(0)
+        quantise_x(0, 0, False)
+        quantise_x(1, 0, True)
+        gather_table(1)
+
+        def message_passes(acc, gate, t, c, stop):
+            half, n0 = divmod(t * P, N_HALF)
+            for a in range(PASSES):
+                s0 = GATES.index(gate) * GATE_COLS + a * N + t * P
+                nc.tensor.matmul_mx(
+                    acc[:],
+                    lhsT=w_codes[gate, half][:, a, n0 : n0 + P].bitcast(FP8X4),
+                    lhsT_scale=w_plane[:, s0 : s0 + P],
+                    rhs=x_codes[a, c][:].bitcast(FP8X4),
+                    rhs_scale=x_plane[a, c][:],
+                    start=(a == 0),
+                    stop=(stop and a == PASSES - 1),
+                )
+
+        def state_pass(acc, gate, t, c, start):
+            s0 = GATES.index(gate) * GATE_COLS + PASSES * N + t * P
+            nc.tensor.matmul_mx(
+                acc[:],
+                lhsT=u_codes[gate][:, 2 * t * P : 2 * (t + 1) * P].bitcast(FP4X4),
+                lhsT_scale=w_plane[:, s0 : s0 + P],
+                rhs=v_codes[c][:].bitcast(FP8X4),
+                rhs_scale=v_plane[c][:],
+                start=start,
+                stop=True,
+            )
+
+        units = [(0, 0), (1, 0), (0, 1), (1, 1), (2, 0), (2, 1), (3, 0), (3, 1)]
+        sums, held = {}, {}
+
+        def products(i):
+            t, c = units[i]
+            sr = psum.tile([P, JC], F32, name="sr")
+            hn = psum.tile([P, JC], F32, name="hn")
+            xn = psum.tile([P, JC], F32, name="xn")
+            sz = psum.tile([P, JC], F32, name="sz")
+            message_passes(sr, "r", t, c, False)
+            state_pass(sr, "r", t, c, False)
+            state_pass(hn, "n", t, c, True)
+            message_passes(xn, "n", t, c, True)
+            message_passes(sz, "z", t, c, False)
+            state_pass(sz, "z", t, c, False)
+            tr = work.tile([P, JC], F32, name="tr")
+            tz = work.tile([P, JC], F32, name="tz")
+            nc.scalar.activation(tr[:], sr[:], ACT.Tanh, bias=half_bias["r"][:, t : t + 1], scale=0.5)
+            nc.scalar.activation(tz[:], sz[:], ACT.Tanh, bias=half_bias["z"][:, t : t + 1], scale=0.5)
+            sums[i] = (hn, xn, tr, tz)
+
+        def reset_product(i):
+            hn, xn, tr, tz = sums[i]
+            rh2 = work.tile([P, JC], F32, name="rh2")
+            nc.vector.scalar_tensor_tensor(rh2[:], tr[:], 1.0, hn[:], ALU.add, ALU.mult)
+            held[i, "rh2"] = rh2
+
+        def candidate(i):
+            t, c = units[i]
+            hn, xn, tr, tz = sums[i]
+            pre = work.tile([P, JC], F32, name="pre")
+            nc.vector.scalar_tensor_tensor(pre[:], held[i, "rh2"][:], 0.5, xn[:], ALU.mult, ALU.add)
+            cd = work.tile([P, JC], F32, name="cd")
+            nc.scalar.activation(cd[:], pre[:], ACT.Tanh, bias=bias["n"][:, t : t + 1])
+            held[i, "cd"] = cd
+
+        def difference(i):
+            t, c = units[i]
+            d = work.tile([P, JC], F32, name="d")
+            nc.vector.tensor_tensor(d[:], state[t][:].indirect(listed(c)), held[i, "cd"][:], ALU.subtract)
+            held[i, "d"] = d
+
+        def gated(i):
+            e = work.tile([P, JC], F32, name="e")
+            nc.vector.scalar_tensor_tensor(e[:], sums[i][3][:], 1.0, held[i, "d"][:], ALU.subtract, ALU.mult)
+            held[i, "e"] = e
+
+        def blend(i):
+            f = work.tile([P, JC], F32, name="f")
+            nc.vector.scalar_tensor_tensor(f[:], held[i, "e"][:], -0.5, held[i, "cd"][:], ALU.mult, ALU.add)
+            held[i, "f"] = f
+
+        def put(i):
+            t, c = units[i]
+            page = pages[t % 2]
+            nc.vector.tensor_tensor(page[:].indirect(listed(c)), held[i, "f"][:], weight[c][:], ALU.mult)
+            if c == J_CHUNKS - 1:
+                nc.sync.dma_start(out[t * P : (t + 1) * P, :], page[:])
+
+        products(0)
+        products(1)
+        quantise_x(0, 1, False)
+        quantise_x(1, 1, False)
+        reset_product(0)
+        candidate(0)
+        last = len(units) - 1
+        for i in range(len(units)):
+            if i < last:
+                reset_product(i + 1)
+            difference(i)
+            if i < last:
+                candidate(i + 1)
+            if i + 2 <= last:
+                products(i + 2)
+            gated(i)
+            if i > 0:
+                put(i - 1)
+            blend(i)
+        put(last)

@@ -1,6 +1,7 @@
 from contextlib import ExitStack
 
 import concourse.mybir as mybir
+from concourse.masks import make_identity
 
 K, M, N, T, J = 1024, 512, 512, 2048, 1024
 FLOPS = 2 * 3 * (K + M) * N * J
@@ -42,49 +43,55 @@ def tile_list_tgn_gru_kernel(
         keep = ctx.enter_context(tc.tile_pool(name="keep", bufs=1))
         work = ctx.enter_context(tc.tile_pool(name="work", bufs=3))
         psum = ctx.enter_context(tc.psum_pool(name="psum", bufs=2))
+        identity = keep.tile([P, P], F32, name="identity")
+        make_identity(nc, identity[:])
 
         offsets = keep.tile([P, J // 16], U16, name="offsets")
-        nc.sync.dma_start(offsets[:], offs)
 
         def listed(c):
             return offsets[:, c * JC // 16 : (c + 1) * JC // 16]
 
-        tab_plane = keep.tile([P, T], U8, name="tab_plane", align_bytes=64)
-        nc.vector.memset(tab_plane[:].bitcast(I32), 0)
-        for q in range(4):
-            nc.gpsimd.dma_start(
-                tab_plane[32 * q : 32 * q + 4, :].bitcast(I32), tab_scales[0, 4 * q : 4 * q + 4, :].bitcast(I32)
-            )
         GATE_COLS = (PASSES + 1) * N
-        w_plane = keep.tile([P, len(GATES) * GATE_COLS], U8, name="w_plane", align_bytes=64)
+        PLANE_COLS = len(GATES) * GATE_COLS
+        tab_plane = keep.tile([P, T], U8, name="tab_plane", align_bytes=64)
+        w_plane = keep.tile([P, PLANE_COLS], U8, name="w_plane", align_bytes=64)
+        nc.vector.memset(tab_plane[:].bitcast(I32), 0)
         nc.vector.memset(w_plane[:].bitcast(I32), 0)
-        w_rows = keep.tile([16, len(GATES) * GATE_COLS // 4], I32, name="w_rows")
-
-        def load_w_scales(gate):
-            c0 = GATES.index(gate) * GATE_COLS // 4
+        rows16 = keep.tile([16, PLANE_COLS // 4], I32, name="rows16")
+        for g, gate in enumerate(GATES):
+            c0 = g * GATE_COLS // 4
+            c1 = c0 + PASSES * N // 4
             nc.sync.dma_start(
-                w_rows[:, c0 : c0 + PASSES * N // 4].rearrange("q (a n) -> q a n", a=PASSES),
+                rows16[:, c0:c1].rearrange("q (a n) -> q a n", a=PASSES),
                 w_scales[gate].bitcast(I32).rearrange("a q n -> q a n"),
             )
+            nc.sync.dma_start(rows16[:, c1 : c1 + N // 4], u_scales[gate][0].bitcast(I32))
+        nc.sync.dma_start(offsets[:], offs)
+        tab = keep.tile([P, T], I32, name="tab", align_bytes=64)
+        nc.sync.dma_start(tab[:], tab_words[0].rearrange("p t i -> p (t i)").bitcast(I32))
+        for q in range(4):
+            nc.sync.dma_start(
+                tab_plane[32 * q : 32 * q + 4, :].bitcast(I32), tab_scales[0, 4 * q : 4 * q + 4, :].bitcast(I32)
+            )
+        for q in range(4):
+            nc.sync.dma_start(w_plane[32 * q : 32 * q + 4, :].bitcast(I32), rows16[4 * q : 4 * q + 4, :])
 
-        def load_u_scales(gate):
-            c0 = (GATES.index(gate) * GATE_COLS + PASSES * N) // 4
-            nc.sync.dma_start(w_rows[:, c0 : c0 + N // 4], u_scales[gate][0].bitcast(I32))
-
-        bias, half_bias = {}, {}
-
-        def load_bias(gate):
-            bias[gate] = keep.tile([P, N_TILES], F32, name="bias_" + gate)
-            with nc.allow_non_contiguous_dma(reason="one bias value for each partition and tile"):
-                nc.sync.dma_start(bias[gate][:], biases[gate].rearrange("(t p) -> p t", p=P))
-            if gate != "n":
-                half_bias[gate] = keep.tile([P, N_TILES], F32, name="half_bias_" + gate)
-                nc.scalar.mul(half_bias[gate][:], bias[gate][:], 0.5)
+        vec_rows = keep.tile([P, P], F32, name="vec_rows")
+        nc.gpsimd.memset(vec_rows[:], 0.0)
+        row = {"r": 0, "z": N_TILES, "n": 2 * N_TILES}
+        for gate in GATES:
+            nc.gpsimd.dma_start(vec_rows[row[gate] : row[gate] + N_TILES, :], biases[gate].rearrange("(t p) -> t p", p=P))
+        vec_turned = psum.tile([P, P], F32, name="vec_turned", tag="hw_turned", bufs=1)
+        nc.tensor.transpose(vec_turned[:], vec_rows[:], identity[:])
+        halved = keep.tile([P, row["n"]], F32, name="halved")
+        doubled = keep.tile([P, N_TILES], F32, name="doubled")
+        nc.scalar.mul(halved[:], vec_turned[:, 0 : row["n"]], 0.5)
+        nc.scalar.mul(doubled[:], vec_turned[:, row["n"] : row["n"] + N_TILES], 2.0)
+        bias = {"r": halved[:, 0:N_TILES], "z": halved[:, N_TILES : 2 * N_TILES], "n": doubled[:]}
 
         pages = [keep.tile([P, T], F32, name="page%d" % i) for i in range(2)]
         for page in pages:
-            nc.vector.memset(page[:, 0 : T // 2 - 1], 0.0)
-            nc.vector.memset(page[:, T // 2 - 1 : T], 0.0)
+            nc.vector.memset(page[:], 0.0)
 
         x_raw, w_codes, u_codes, state, weight = {}, {}, {}, {}, {}
 
@@ -110,32 +117,23 @@ def tile_list_tgn_gru_kernel(
             weight[c] = keep.tile([P, JC], F32, name="weight%d" % c)
             nc.sync.dma_start(weight[c][:], wgo[:, c * JC : (c + 1) * JC])
 
-        tab = keep.tile([P, T], I32, name="tab", align_bytes=64)
         load_x(0, 0)
-        load_w_scales("r")
-        load_u_scales("r")
-        nc.sync.dma_start(tab[:], tab_words[0].rearrange("p t i -> p (t i)").bitcast(I32))
-        load_w_scales("n")
-        load_u_scales("n")
-        load_w_scales("z")
-        load_u_scales("z")
         load_x(1, 0)
-        for q in range(4):
-            nc.gpsimd.dma_start(w_plane[32 * q : 32 * q + 4, :].bitcast(I32), w_rows[4 * q : 4 * q + 4, :])
-        for gate in GATES:
-            load_w(gate, 0)
-            load_u(gate)
-        load_bias("r")
-        load_state(0)
-        load_bias("n")
-        load_bias("z")
+        load_w("r", 0)
+        load_u("r")
+        load_u("n")
+        load_w("n", 0)
         load_weight(0)
+        load_state(0)
+        load_u("z")
+        load_w("z", 0)
+        load_weight(1)
+        load_state(1)
         load_x(0, 1)
         load_x(1, 1)
-        load_state(1)
-        load_weight(1)
-        for gate in GATES:
-            load_w(gate, 1)
+        load_w("r", 1)
+        load_w("n", 1)
+        load_w("z", 1)
         load_state(2)
         load_state(3)
 
@@ -148,7 +146,8 @@ def tile_list_tgn_gru_kernel(
             if on_vector:
                 nc.vector.tensor_copy(dst, src)
             else:
-                nc.scalar.copy(dst, src)
+                for g in range(0, JC // 4, JC // 16):
+                    nc.scalar.copy(dst[:, g : g + JC // 16], src[:, g : g + JC // 16])
             x_codes[a, c] = keep.tile([P, JC], U32, name="x_codes%d%d" % (a, c), align_bytes=64)
             x_plane[a, c] = keep.tile([P, JC], U8, name="x_plane%d%d" % (a, c), align_bytes=64)
             nc.vector.quantize_mx(
@@ -195,79 +194,111 @@ def tile_list_tgn_gru_kernel(
         units = [(0, 0), (1, 0), (0, 1), (1, 1), (2, 0), (2, 1), (3, 0), (3, 1)]
         sums, held = {}, {}
 
+        BLOCKS = JC // P
+
+        def turned_sum(acc, parts):
+            for k, part in enumerate(parts):
+                for b in range(BLOCKS):
+                    cols = slice(b * P, (b + 1) * P)
+                    nc.tensor.matmul(
+                        acc[:, cols], lhsT=part[:, cols], rhs=identity[:], is_transpose=True,
+                        start=(k == 0 and b == 0), stop=(k == len(parts) - 1 and b == BLOCKS - 1),
+                    )
+
+        half_weight = {}
+
+        def weight_columns(c):
+            turned = psum.tile([P, JC], F32, name="weight_turned", tag="hw_turned", bufs=1)
+            turned_sum(turned, [weight[c]])
+            half_weight[c] = keep.tile([P, BLOCKS], F32, name="half_weight%d" % c)
+            nc.scalar.mul(half_weight[c][:], turned[:, 0:JC:P], 0.5)
+
         def products(i):
             t, c = units[i]
-            sr = psum.tile([P, JC], F32, name="sr")
-            hn = psum.tile([P, JC], F32, name="hn")
-            xn = psum.tile([P, JC], F32, name="xn")
-            sz = psum.tile([P, JC], F32, name="sz")
+            sr = psum.tile([P, JC], F32, name="sr", tag="gate")
             message_passes(sr, "r", t, c, False)
             state_pass(sr, "r", t, c, False)
+            r = work.tile([P, JC], F32, name="r")
+            nc.scalar.activation(r[:], sr[:], ACT.Tanh, bias=bias["r"][:, t : t + 1], scale=0.5)
+            hn = psum.tile([P, JC], F32, name="hn")
             state_pass(hn, "n", t, c, True)
+            xn = psum.tile([P, JC], F32, name="xn", tag="gate")
             message_passes(xn, "n", t, c, True)
+            xb = work.tile([P, JC], F32, name="xb")
+            nc.scalar.activation(xb[:], xn[:], ACT.Identity, bias=bias["n"][:, t : t + 1], scale=2.0)
+            held[i, "hn"], held[i, "r"], held[i, "xb"] = hn, r, xb
+
+        def update_gate(i):
+            t, c = units[i]
+            sz = psum.tile([P, JC], F32, name="sz", tag="gate")
             message_passes(sz, "z", t, c, False)
             state_pass(sz, "z", t, c, False)
-            tr = work.tile([P, JC], F32, name="tr")
-            tz = work.tile([P, JC], F32, name="tz")
-            nc.scalar.activation(tr[:], sr[:], ACT.Tanh, bias=half_bias["r"][:, t : t + 1], scale=0.5)
-            nc.scalar.activation(tz[:], sz[:], ACT.Tanh, bias=half_bias["z"][:, t : t + 1], scale=0.5)
-            sums[i] = (hn, xn, tr, tz)
+            z = work.tile([P, JC], F32, name="z")
+            nc.scalar.activation(z[:], sz[:], ACT.Tanh, bias=bias["z"][:, t : t + 1], scale=0.5)
+            held[i, "z"] = z
 
-        def reset_product(i):
-            hn, xn, tr, tz = sums[i]
-            rh2 = work.tile([P, JC], F32, name="rh2")
-            nc.vector.scalar_tensor_tensor(rh2[:], tr[:], 1.0, hn[:], ALU.add, ALU.mult)
-            held[i, "rh2"] = rh2
+        def weighted_state(i):
+            t, c = units[i]
+            hw = work.tile([P, JC], F32, name="hw", bufs=8)
+            nc.vector.tensor_tensor(hw[:], state[t][:].indirect(listed(c)), weight[c][:], ALU.mult)
+            held[i, "hw"] = hw
+
+        def turned_state(i):
+            hw = held[i, "hw"]
+            hw_turned = psum.tile([P, JC], F32, name="hw_turned", bufs=1)
+            turned_sum(hw_turned, [hw])
+            minus_hw = work.tile([P, JC], F32, name="minus_hw", bufs=1)
+            nc.scalar.activation(minus_hw[:], hw_turned[:], ACT.Copy, scale=-0.5)
+            held[i, "minus_hw"] = minus_hw
 
         def candidate(i):
             t, c = units[i]
-            hn, xn, tr, tz = sums[i]
-            pre = work.tile([P, JC], F32, name="pre")
-            nc.vector.scalar_tensor_tensor(pre[:], held[i, "rh2"][:], 0.5, xn[:], ALU.mult, ALU.add)
+            rh = work.tile([P, JC], F32, name="rh")
+            nc.vector.scalar_tensor_tensor(rh[:], held[i, "r"][:], 1.0, held[i, "hn"][:], ALU.add, ALU.mult)
+            pre = psum.tile([P, JC], F32, name="pre", bufs=1)
+            turned_sum(pre, [held[i, "xb"], rh])
             cd = work.tile([P, JC], F32, name="cd")
-            nc.scalar.activation(cd[:], pre[:], ACT.Tanh, bias=bias["n"][:, t : t + 1])
-            held[i, "cd"] = cd
-
-        def difference(i):
-            t, c = units[i]
-            d = work.tile([P, JC], F32, name="d")
-            nc.vector.tensor_tensor(d[:], state[t][:].indirect(listed(c)), held[i, "cd"][:], ALU.subtract)
-            held[i, "d"] = d
+            nc.scalar.activation(cd[:], pre[:], ACT.Tanh, scale=0.5)
+            cdw = work.tile([P, JC], F32, name="cdw")
+            for b in range(BLOCKS):
+                cols = slice(b * P, (b + 1) * P)
+                nc.scalar.activation(cdw[:, cols], cd[:, cols], ACT.Copy, scale=half_weight[c][:, b : b + 1])
+            held[i, "cdw"] = cdw
 
         def gated(i):
-            e = work.tile([P, JC], F32, name="e")
-            nc.vector.scalar_tensor_tensor(e[:], sums[i][3][:], 1.0, held[i, "d"][:], ALU.subtract, ALU.mult)
+            step = psum.tile([P, JC], F32, name="step")
+            turned_sum(step, [held[i, "minus_hw"], held[i, "cdw"]])
+            e = held[i + 1, "r"] if i + 1 < len(units) else work.tile([P, JC], F32, name="r")
+            nc.vector.scalar_tensor_tensor(e[:], held[i, "z"][:], 1.0, step[:], ALU.add, ALU.mult)
             held[i, "e"] = e
-
-        def blend(i):
-            f = work.tile([P, JC], F32, name="f")
-            nc.vector.scalar_tensor_tensor(f[:], held[i, "e"][:], -0.5, held[i, "cd"][:], ALU.mult, ALU.add)
-            held[i, "f"] = f
 
         def put(i):
             t, c = units[i]
             page = pages[t % 2]
-            nc.vector.tensor_tensor(page[:].indirect(listed(c)), held[i, "f"][:], weight[c][:], ALU.mult)
+            nc.vector.tensor_tensor(page[:].indirect(listed(c)), held[i, "e"][:], held[i, "hw"][:], ALU.add)
             if c == J_CHUNKS - 1:
                 nc.sync.dma_start(out[t * P : (t + 1) * P, :], page[:])
 
+        count = len(units)
         products(0)
+        weight_columns(0)
+        weighted_state(0)
+        turned_state(0)
+        candidate(0)
         products(1)
+        update_gate(0)
+        weighted_state(1)
+        weight_columns(1)
         quantise_x(0, 1, False)
         quantise_x(1, 1, False)
-        reset_product(0)
-        candidate(0)
-        last = len(units) - 1
-        for i in range(len(units)):
-            if i < last:
-                reset_product(i + 1)
-            difference(i)
-            if i < last:
+        for i in range(count):
+            if i + 1 < count:
                 candidate(i + 1)
-            if i + 2 <= last:
-                products(i + 2)
             gated(i)
-            if i > 0:
-                put(i - 1)
-            blend(i)
-        put(last)
+            if i + 1 < count:
+                turned_state(i + 1)
+                update_gate(i + 1)
+            if i + 2 < count:
+                products(i + 2)
+                weighted_state(i + 2)
+            put(i)

@@ -57,7 +57,7 @@ def tile_list_tgn_gru_kernel(
         w_plane = keep.tile([P, PLANE_COLS], U8, name="w_plane", align_bytes=64)
         nc.vector.memset(tab_plane[:].bitcast(I32), 0)
         nc.vector.memset(w_plane[:].bitcast(I32), 0)
-        rows16 = keep.tile([16, PLANE_COLS // 4], I32, name="rows16")
+        rows16 = keep.tile([32, PLANE_COLS // 4], I32, name="rows16")[16:32, :]
         for g, gate in enumerate(GATES):
             c0 = g * GATE_COLS // 4
             c1 = c0 + PASSES * N // 4
@@ -96,7 +96,7 @@ def tile_list_tgn_gru_kernel(
         x_raw, w_codes, u_codes, state, weight = {}, {}, {}, {}, {}
 
         def load_x(a, c):
-            x_raw[a, c] = keep.tile([P, PACK, JC], F32, name="x_raw%d%d" % (a, c))
+            x_raw[a, c] = keep.tile([P, PACK, JC], F32, name="x_raw%d%d" % (a, c), tag="x_raw%d%d" % (a, c))
             rows = x[a * K_PASS : (a + 1) * K_PASS, c * JC : (c + 1) * JC]
             nc.sync.dma_start(x_raw[a, c][:], rows.rearrange("(p i) j -> p i j", i=PACK))
 
@@ -233,7 +233,7 @@ def tile_list_tgn_gru_kernel(
             sz = psum.tile([P, JC], F32, name="sz", tag="gate")
             message_passes(sz, "z", t, c, False)
             state_pass(sz, "z", t, c, False)
-            z = work.tile([P, JC], F32, name="z")
+            z = late[:, 2, :] if i == 1 else work.tile([P, JC], F32, name="z")[:]
             nc.scalar.activation(z[:], sz[:], ACT.Tanh, bias=bias["z"][:, t : t + 1], scale=0.5)
             held[i, "z"] = z
 
@@ -247,7 +247,7 @@ def tile_list_tgn_gru_kernel(
             hw = held[i, "hw"]
             hw_turned = psum.tile([P, JC], F32, name="hw_turned", bufs=1)
             turned_sum(hw_turned, [hw])
-            minus_hw = work.tile([P, JC], F32, name="minus_hw", bufs=1)
+            minus_hw = late[:, 1, :] if i == 1 else work.tile([P, JC], F32, name="minus_hw", bufs=1)[:]
             nc.scalar.activation(minus_hw[:], hw_turned[:], ACT.Copy, scale=-0.5)
             held[i, "minus_hw"] = minus_hw
 
@@ -257,7 +257,7 @@ def tile_list_tgn_gru_kernel(
             nc.vector.scalar_tensor_tensor(rh[:], held[i, "r"][:], 1.0, held[i, "hn"][:], ALU.add, ALU.mult)
             pre = psum.tile([P, JC], F32, name="pre", bufs=1)
             turned_sum(pre, [held[i, "xb"], rh])
-            cd = work.tile([P, JC], F32, name="cd")
+            cd = late[:, 0, :] if i == 1 else work.tile([P, JC], F32, name="cd")[:]
             nc.scalar.activation(cd[:], pre[:], ACT.Tanh, scale=0.5)
             cdw = work.tile([P, JC], F32, name="cdw")
             for b in range(BLOCKS):
@@ -268,6 +268,10 @@ def tile_list_tgn_gru_kernel(
         def gated(i):
             step = psum.tile([P, JC], F32, name="step")
             turned_sum(step, [held[i, "minus_hw"], held[i, "cdw"]])
+            held[i, "step"] = step
+
+        def gated_product(i):
+            step = held[i, "step"]
             e = held[i + 1, "r"] if i + 1 < len(units) else work.tile([P, JC], F32, name="r")
             nc.vector.scalar_tensor_tensor(e[:], held[i, "z"][:], 1.0, step[:], ALU.add, ALU.mult)
             held[i, "e"] = e
@@ -291,13 +295,14 @@ def tile_list_tgn_gru_kernel(
         weight_columns(1)
         quantise_x(0, 1, False)
         quantise_x(1, 1, False)
+        late = keep.tile([P, 3, JC], F32, name="late", tag="x_raw11")
         for i in range(count):
-            if i + 1 < count:
-                candidate(i + 1)
             gated(i)
             if i + 1 < count:
                 turned_state(i + 1)
                 update_gate(i + 1)
+                candidate(i + 1)
+            gated_product(i)
             if i + 2 < count:
                 products(i + 2)
                 weighted_state(i + 2)

from contextlib import ExitStack

import concourse.mybir as mybir
from concourse.masks import make_identity

K, M, N, T, J = 1024, 512, 512, 2048, 1024
FLOPS = 2 * 3 * (K + M) * N * J

F32 = mybir.dt.float32
BF16 = mybir.dt.bfloat16
I32 = mybir.dt.int32
U32 = mybir.dt.uint32
U16 = mybir.dt.uint16
U8 = mybir.dt.uint8
FP8X4 = mybir.dt.float8_e4m3fn_x4
FP4X4 = mybir.dt.float4_e2m1fn_x4
ALU = mybir.AluOpType
ACT = mybir.ActivationFunctionType

P = 128
PACK = 4
K_PASS = P * PACK
PASSES = K // K_PASS
JC = 512
J_CHUNKS = J // JC
N_TILES = N // P
N_HALF = N // 2
GATES = ("r", "n", "z")


def tile_list_tgn_gru_kernel(
    tc, x, tab_words, tab_scales, wz_words, wz_scales, uz_words, uz_scales, wr_words, wr_scales, ur_words,
    ur_scales, wn_words, wn_scales, un_words, un_scales, bz, br, bn, hT, wgo, offs, out,
):
    nc = tc.nc
    w_words = {"r": wr_words, "n": wn_words, "z": wz_words}
    w_scales = {"r": wr_scales, "n": wn_scales, "z": wz_scales}
    u_words = {"r": ur_words, "n": un_words, "z": uz_words}
    u_scales = {"r": ur_scales, "n": un_scales, "z": uz_scales}
    biases = {"r": br, "n": bn, "z": bz}

    with ExitStack() as ctx:
        keep = ctx.enter_context(tc.tile_pool(name="keep", bufs=1))
        work = ctx.enter_context(tc.tile_pool(name="work", bufs=3))
        psum = ctx.enter_context(tc.psum_pool(name="psum", bufs=2))
        identity = keep.tile([P, P], F32, name="identity")
        make_identity(nc, identity[:])

        offsets = keep.tile([P, J // 16], U16, name="offsets")

        def listed(c):
            return offsets[:, c * JC // 16 : (c + 1) * JC // 16]

        GATE_COLS = (PASSES + 1) * N
        PLANE_COLS = len(GATES) * GATE_COLS
        tab_plane = keep.tile([P, T], U8, name="tab_plane", align_bytes=64)
        w_plane = keep.tile([P, PLANE_COLS], U8, name="w_plane", align_bytes=64)
        nc.vector.memset(tab_plane[:].bitcast(I32), 0)
        nc.vector.memset(w_plane[:].bitcast(I32), 0)
        rows16 = keep.tile([32, PLANE_COLS // 4], I32, name="rows16")[16:32, :]
        for g, gate in enumerate(GATES):
            c0 = g * GATE_COLS // 4
            c1 = c0 + PASSES * N // 4
            nc.sync.dma_start(
                rows16[:, c0:c1].rearrange("q (a n) -> q a n", a=PASSES),
                w_scales[gate].bitcast(I32).rearrange("a q n -> q a n"),
            )
            nc.sync.dma_start(rows16[:, c1 : c1 + N // 4], u_scales[gate][0].bitcast(I32))
        nc.sync.dma_start(offsets[:], offs)
        tab = keep.tile([P, T], I32, name="tab", align_bytes=64)
        nc.sync.dma_start(tab[:], tab_words[0].rearrange("p t i -> p (t i)").bitcast(I32))
        for q in range(4):
            nc.sync.dma_start(
                tab_plane[32 * q : 32 * q + 4, :].bitcast(I32), tab_scales[0, 4 * q : 4 * q + 4, :].bitcast(I32)
            )
        for q in range(4):
            nc.sync.dma_start(w_plane[32 * q : 32 * q + 4, :].bitcast(I32), rows16[4 * q : 4 * q + 4, :])

        vec_rows = keep.tile([P, P], F32, name="vec_rows")
        nc.gpsimd.memset(vec_rows[:], 0.0)
        row = {"r": 0, "z": N_TILES, "n": 2 * N_TILES}
        for gate in GATES:
            nc.gpsimd.dma_start(vec_rows[row[gate] : row[gate] + N_TILES, :], biases[gate].rearrange("(t p) -> t p", p=P))
        vec_turned = psum.tile([P, P], F32, name="vec_turned", tag="hw_turned", bufs=1)
        nc.tensor.transpose(vec_turned[:], vec_rows[:], identity[:])
        halved = keep.tile([P, row["n"]], F32, name="halved")
        doubled = keep.tile([P, N_TILES], F32, name="doubled")
        nc.scalar.mul(halved[:], vec_turned[:, 0 : row["n"]], 0.5)
        nc.scalar.mul(doubled[:], vec_turned[:, row["n"] : row["n"] + N_TILES], 2.0)
        bias = {"r": halved[:, 0:N_TILES], "z": halved[:, N_TILES : 2 * N_TILES], "n": doubled[:]}

        pages = [keep.tile([P, T], F32, name="page%d" % i) for i in range(2)]
        for page in pages:
            nc.vector.memset(page[:], 0.0)

        x_raw, w_codes, u_codes, state, weight = {}, {}, {}, {}, {}

        def load_x(a, c):
            x_raw[a, c] = keep.tile([P, PACK, JC], F32, name="x_raw%d%d" % (a, c), tag="x_raw%d%d" % (a, c))
            rows = x[a * K_PASS : (a + 1) * K_PASS, c * JC : (c + 1) * JC]
            nc.sync.dma_start(x_raw[a, c][:], rows.rearrange("(p i) j -> p i j", i=PACK))

        def load_w(gate, half):
            w_codes[gate, half] = keep.tile([P, PASSES, N_HALF], I32, name="w_%s%d" % (gate, half), align_bytes=64)
            words = w_words[gate].rearrange("a p n i -> p a (n i)").bitcast(I32)
            nc.sync.dma_start(w_codes[gate, half][:], words[:, :, half * N_HALF : (half + 1) * N_HALF])

        def load_u(gate):
            u_codes[gate] = keep.tile([P, 2 * N], U8, name="u_" + gate, align_bytes=64)
            nc.sync.dma_start(u_codes[gate][:].bitcast(I32), u_words[gate][0].bitcast(I32))

        def load_state(t):
            state[t] = keep.tile([P, T], F32, name="state%d" % t)
            nc.sync.dma_start(state[t][:], hT[t * P : (t + 1) * P, :])

        def load_weight(c):
            weight[c] = keep.tile([P, JC], F32, name="weight%d" % c)
            nc.sync.dma_start(weight[c][:], wgo[:, c * JC : (c + 1) * JC])

        load_x(0, 0)
        load_x(1, 0)
        load_w("r", 0)
        load_u("r")
        load_u("n")
        load_w("n", 0)
        load_weight(0)
        load_state(0)
        load_u("z")
        load_w("z", 0)
        load_weight(1)
        load_state(1)
        load_x(0, 1)
        load_x(1, 1)
        load_w("r", 1)
        load_w("n", 1)
        load_w("z", 1)
        load_state(2)
        load_state(3)

        x_codes, x_plane, v_codes, v_plane = {}, {}, {}, {}

        def quantise_x(a, c, on_vector):
            grouped = keep.tile([P, JC, PACK], BF16, name="grouped%d%d" % (a, c), align_bytes=64)
            dst = grouped[:].rearrange("p (g i) t -> p g t i", i=4)
            src = x_raw[a, c][:].rearrange("p t (g i) -> p g t i", i=4)
            if on_vector:
                nc.vector.tensor_copy(dst, src)
            else:
                for g in range(0, JC // 4, JC // 16):
                    nc.scalar.copy(dst[:, g : g + JC // 16], src[:, g : g + JC // 16])
            x_codes[a, c] = keep.tile([P, JC], U32, name="x_codes%d%d" % (a, c), align_bytes=64)
            x_plane[a, c] = keep.tile([P, JC], U8, name="x_plane%d%d" % (a, c), align_bytes=64)
            nc.vector.quantize_mx(
                x_codes[a, c][:].bitcast(FP8X4), x_plane[a, c][:], grouped[:].rearrange("p j t -> p (j t)")
            )

        def gather_table(c):
            v_codes[c] = keep.tile([P, JC], U32, name="v_codes%d" % c, align_bytes=64)
            v_plane[c] = keep.tile([P, JC], U8, name="v_plane%d" % c, align_bytes=64)
            nc.vector.tensor_copy(v_codes[c][:], tab[:].bitcast(U32).indirect(listed(c)))
            nc.vector.tensor_copy(v_plane[c][:], tab_plane[:].indirect(listed(c)))

        gather_table(0)
        quantise_x(0, 0, False)
        quantise_x(1, 0, True)
        gather_table(1)

        def message_passes(acc, gate, t, c, stop):
            half, n0 = divmod(t * P, N_HALF)
            for a in range(PASSES):
                s0 = GATES.index(gate) * GATE_COLS + a * N + t * P
                nc.tensor.matmul_mx(
                    acc[:],
                    lhsT=w_codes[gate, half][:, a, n0 : n0 + P].bitcast(FP8X4),
                    lhsT_scale=w_plane[:, s0 : s0 + P],
                    rhs=x_codes[a, c][:].bitcast(FP8X4),
                    rhs_scale=x_plane[a, c][:],
                    start=(a == 0),
                    stop=(stop and a == PASSES - 1),
                )

        def state_pass(acc, gate, t, c, start):
            s0 = GATES.index(gate) * GATE_COLS + PASSES * N + t * P
            nc.tensor.matmul_mx(
                acc[:],
                lhsT=u_codes[gate][:, 2 * t * P : 2 * (t + 1) * P].bitcast(FP4X4),
                lhsT_scale=w_plane[:, s0 : s0 + P],
                rhs=v_codes[c][:].bitcast(FP8X4),
                rhs_scale=v_plane[c][:],
                start=start,
                stop=True,
            )

        units = [(0, 0), (1, 0), (0, 1), (1, 1), (2, 0), (2, 1), (3, 0), (3, 1)]
        sums, held = {}, {}

        BLOCKS = JC // P

        def turned_sum(acc, parts):
            for k, part in enumerate(parts):
                for b in range(BLOCKS):
                    cols = slice(b * P, (b + 1) * P)
                    nc.tensor.matmul(
                        acc[:, cols], lhsT=part[:, cols], rhs=identity[:], is_transpose=True,
                        start=(k == 0 and b == 0), stop=(k == len(parts) - 1 and b == BLOCKS - 1),
                    )

        half_weight = {}

        def weight_columns(c):
            turned = psum.tile([P, JC], F32, name="weight_turned", tag="hw_turned", bufs=1)
            turned_sum(turned, [weight[c]])
            half_weight[c] = keep.tile([P, BLOCKS], F32, name="half_weight%d" % c)
            nc.scalar.mul(half_weight[c][:], turned[:, 0:JC:P], 0.5)

        def products(i):
            t, c = units[i]
            sr = psum.tile([P, JC], F32, name="sr", tag="gate")
            message_passes(sr, "r", t, c, False)
            state_pass(sr, "r", t, c, False)
            r = work.tile([P, JC], F32, name="r")
            nc.scalar.activation(r[:], sr[:], ACT.Tanh, bias=bias["r"][:, t : t + 1], scale=0.5)
            hn = psum.tile([P, JC], F32, name="hn")
            state_pass(hn, "n", t, c, True)
            xn = psum.tile([P, JC], F32, name="xn", tag="gate")
            message_passes(xn, "n", t, c, True)
            xb = work.tile([P, JC], F32, name="xb")
            nc.scalar.activation(xb[:], xn[:], ACT.Identity, bias=bias["n"][:, t : t + 1], scale=2.0)
            held[i, "hn"], held[i, "r"], held[i, "xb"] = hn, r, xb

        def update_gate(i):
            t, c = units[i]
            sz = psum.tile([P, JC], F32, name="sz", tag="gate")
            message_passes(sz, "z", t, c, False)
            state_pass(sz, "z", t, c, False)
            z = late[:, 2, :] if i == 1 else work.tile([P, JC], F32, name="z")[:]
            nc.scalar.activation(z[:], sz[:], ACT.Tanh, bias=bias["z"][:, t : t + 1], scale=0.5)
            held[i, "z"] = z

        def weighted_state(i):
            t, c = units[i]
            hw = work.tile([P, JC], F32, name="hw", bufs=8)
            nc.vector.tensor_tensor(hw[:], state[t][:].indirect(listed(c)), weight[c][:], ALU.mult)
            held[i, "hw"] = hw

        def turned_state(i):
            hw = held[i, "hw"]
            hw_turned = psum.tile([P, JC], F32, name="hw_turned", bufs=1)
            turned_sum(hw_turned, [hw])
            minus_hw = late[:, 1, :] if i == 1 else work.tile([P, JC], F32, name="minus_hw", bufs=1)[:]
            nc.scalar.activation(minus_hw[:], hw_turned[:], ACT.Copy, scale=-0.5)
            held[i, "minus_hw"] = minus_hw

        def candidate(i):
            t, c = units[i]
            rh = work.tile([P, JC], F32, name="rh")
            nc.vector.scalar_tensor_tensor(rh[:], held[i, "r"][:], 1.0, held[i, "hn"][:], ALU.add, ALU.mult)
            pre = psum.tile([P, JC], F32, name="pre", bufs=1)
            turned_sum(pre, [held[i, "xb"], rh])
            cd = late[:, 0, :] if i == 1 else work.tile([P, JC], F32, name="cd")[:]
            nc.scalar.activation(cd[:], pre[:], ACT.Tanh, scale=0.5)
            cdw = work.tile([P, JC], F32, name="cdw")
            for b in range(BLOCKS):
                cols = slice(b * P, (b + 1) * P)
                nc.scalar.activation(cdw[:, cols], cd[:, cols], ACT.Copy, scale=half_weight[c][:, b : b + 1])
            held[i, "cdw"] = cdw

        def gated(i):
            step = psum.tile([P, JC], F32, name="step")
            turned_sum(step, [held[i, "minus_hw"], held[i, "cdw"]])
            held[i, "step"] = step

        def gated_product(i):
            step = held[i, "step"]
            e = held[i + 1, "r"] if i + 1 < len(units) else work.tile([P, JC], F32, name="r")
            nc.vector.scalar_tensor_tensor(e[:], held[i, "z"][:], 1.0, step[:], ALU.add, ALU.mult)
            held[i, "e"] = e

        def put(i):
            t, c = units[i]
            page = pages[t % 2]
            nc.vector.tensor_tensor(page[:].indirect(listed(c)), held[i, "e"][:], held[i, "hw"][:], ALU.add)
            if c == J_CHUNKS - 1:
                nc.sync.dma_start(out[t * P : (t + 1) * P, :], page[:])

        count = len(units)
        products(0)
        weight_columns(0)
        weighted_state(0)
        turned_state(0)
        candidate(0)
        products(1)
        update_gate(0)
        weighted_state(1)
        weight_columns(1)
        quantise_x(0, 1, False)
        quantise_x(1, 1, False)
        late = keep.tile([P, 3, JC], F32, name="late", tag="x_raw11")
        for i in range(count):
            gated(i)
            if i + 1 < count:
                turned_state(i + 1)
                update_gate(i + 1)
                candidate(i + 1)
            gated_product(i)
            if i + 2 < count:
                products(i + 2)
                weighted_state(i + 2)
            put(i)
